import numpy as np, ml_dtypes
CORES = [3,11,19,27,35,43]
N = 6
import mx_ref
BF = ml_dtypes.bfloat16
def entries(a):
    return np.ascontiguousarray(a.T).reshape(-1)
def table(e):
    return np.ascontiguousarray(np.reshape(e, (-1, 16)).T).astype(np.int32)
def cols(t, e):
    v = np.concatenate([t.reshape(128, -1, 4), np.zeros((128, 1, 4), BF)], axis=1)
    return np.ascontiguousarray(v[:, e]).reshape(128, -1)
def tile(rs):
    return np.stack(rs, axis=2).reshape(128, -1).astype(BF)
def cut(t, i, w=512):
    return t[:, w * i:w * i + w]
def f(rng, *shape):
    return mx_ref.flush((rng.standard_normal(shape, dtype=np.float32) * np.exp2(rng.integers(-2, 3, shape[:-1] + (1,)))).astype(BF))
def wide(rng, *shape, cols=0):
    v = rng.standard_normal(shape, dtype=np.float32) * np.exp2(rng.integers(-12, 13, shape)).astype(np.float32)
    if cols: v *= np.repeat(np.exp2(rng.integers(-cols, cols + 1, shape[:-2] + (1, shape[-1] // 4))) * (rng.random(shape[:-2] + (1, shape[-1] // 4)) > 0.0625), 4, axis=-1).astype(np.float32)
    return mx_ref.flush(v.astype(BF))
T, P, CAPP = 128, 192, 32
BASE = T + 3 * P
def sends(a):
    return entries(a).reshape(3, N, CAPP)
def filled(s, r, t):
    return s[:, :t, r].transpose(1, 0, 2).reshape(-1) >= 0
def lists(rng, how=""):
    s = np.full((N, 3, N, CAPP), -1)
    a = int(rng.integers(0, N)); same = (a, int(rng.integers(0, 3)), (a + int(rng.integers(1, N))) % N)
    for t in range(3):
        for q in range(N):
            got = BASE + np.flatnonzero(filled(s, q, t))
            for r in range(N):
                if q == r: continue
                least = 1 if t == 0 and r == (q + 1) % N else 0
                k = rng.permutation(CAPP)[:CAPP if how == "far" else rng.integers(least, CAPP + 1)]
                e = rng.integers(T + (t - 1) * P if how == "far" and t > 0 else 0, T + t * P, len(k))
                if t > 0:
                    m = (len(k) + 1) // 2; e[:m] = got[rng.integers(0, len(got), m)]
                s[q, t, r, k] = e
                if how == "shared" and (q, t, r) == same: s[q, t, r] = rng.integers(0, T + t * P)
    c = np.zeros((N, 2, 3, P), int)
    for r in range(N):
        for t in range(3):
            low = 2 if how == "skip" and t == 2 else t + 1
            own = T + (low - 1) * P; got = BASE + np.flatnonzero(filled(s, r, low))
            for h in range(2):
                c[r, h, t] = rng.integers(0, own, P)
                if len(got):
                    there = np.ones(P, bool) if how == "far" else rng.random(P) < 0.5
                    c[r, h, t] = np.where(there, got[rng.integers(0, len(got), P)], c[r, h, t])
            if how == "shared":
                one = int(c[r, 0, t, 0]); k = rng.permutation(P)
                c[r, 0, t, k[:P - P // 8]] = one; c[r, 1, t, k[:P // 8]] = one
            if how == "chains":
                c[r, 0, t] = np.arange(P) % T if t == 0 else T + (t - 1) * P + np.arange(P)
                c[r, 1, t] = rng.integers(0, T, P)
    return {"sn": np.stack([table(s[r]) for r in range(N)]), "lc": np.stack([table(c[r, 0]) for r in range(N)]), "rc": np.stack([table(c[r, 1]) for r in range(N)])}
def setup_inputs(rng):
    return {"x": f(rng, N, 128, 4 * T), "wl": np.stack([f(rng, 128, 2048)] * N), "wr": np.stack([f(rng, 128, 2048)] * N), "v": f(rng, N, 128, 512), **lists(rng)}
def setup_inputs_chains(rng):
    return {**setup_inputs(rng), **lists(rng, "chains")}
def setup_inputs_far(rng):
    return {**setup_inputs(rng), **lists(rng, "far")}
def setup_inputs_shared(rng):
    return {**setup_inputs(rng), **lists(rng, "shared")}
def setup_inputs_skip(rng):
    return {**setup_inputs(rng), **lists(rng, "skip")}
def setup_inputs_spread(rng):
    d = setup_inputs(rng); d["x"] = wide(rng, N, 128, 4 * T, cols=8); return d
def check_inputs(d):
    b = []
    for n in ("wl", "wr"):
        if any((d[n][r] != d[n][0]).any() for r in range(N)): b.append(n)
    s = np.stack([sends(d["sn"][r]) for r in range(N)])
    for r in range(N):
        for t in range(3):
            own = np.concatenate([np.ones(T + t * P, bool), np.zeros((3 - t) * P, bool)])
            ok = np.concatenate([own, filled(s, r, t)]); e = s[r, t]
            if e.min() < -1 or e.max() >= len(ok) or not ok[e[e >= 0]].all() or (s[r, t, r] != -1).any(): b.append("sn")
            ok = np.concatenate([own, filled(s, r, t + 1)])
            for n in ("lc", "rc"):
                e = entries(d[n][r])[t * P:t * P + P]
                if e.min() < 0 or e.max() >= len(ok) or not ok[e].all(): b.append(n)
    return b
def reference(x, wl, wr, v, sn, lc, rc):
    WL = [[mx_ref.quantize(np.ascontiguousarray(cut(wl[r], i))) for i in range(4)] for r in range(N)]
    WR = [[mx_ref.quantize(np.ascontiguousarray(cut(wr[r], i))) for i in range(4)] for r in range(N)]
    pool = [x[r] for r in range(N)]; slots = [[] for r in range(N)]
    for t in range(3):
        before = [np.concatenate([pool[r], np.zeros((128, 4 * (3 - t) * P), BF)] + slots[r], axis=1) for r in range(N)]
        for r in range(N):
            for q in range(N): slots[r].append(cols(before[q], sends(sn[q])[t, r]))
        made = []
        for r in range(N):
            known = np.concatenate([before[r]] + slots[r][t * N:], axis=1)
            left = mx_ref.quantize(cols(known, entries(lc[r])[t * P:t * P + P]))
            right = mx_ref.quantize(cols(known, entries(rc[r])[t * P:t * P + P]))
            made.append(tile([np.maximum(mx_ref.matmul(WL[r][i], left) + mx_ref.matmul(WR[r][i], right), np.float32(0)) * np.float32(0.05) for i in range(4)]))
        pool = [np.concatenate([pool[r], made[r]], axis=1) for r in range(N)]
    y = np.zeros((N, 128, P), np.float32)
    for r in range(N):
        y[r] = mx_ref.matmul(mx_ref.quantize(v[r]), mx_ref.quantize(np.ascontiguousarray(pool[r][:, 4 * (T + 2 * P):])))
    return {"y": y}

@@ -1,0 +1,256 @@
+from concourse.bass import DstId, RemoteDMATransfer
+from concourse.mybir import dt, AluOpType, ActivationFunctionType
+
+N, LEAVES, NODES, CAPP, LEVELS = 6, 128, 192, 32, 3
+BASE = LEAVES + LEVELS * NODES
+SENT = (N - 1) * CAPP
+F8 = "float8_e4m3fn_x4"
+KIDS = NODES // 16
+OFFS = SENT // 16
+
+SCRATCH = {
+    "xt": ("sbuf", [128, 4 * LEAVES], "bfloat16"),
+    "wlt": ("sbuf", [128, 2048], "bfloat16"),
+    "wrt": ("sbuf", [128, 2048], "bfloat16"),
+    "vt": ("sbuf", [128, 512], "bfloat16"),
+    "sni": ("sbuf", [128, LEVELS * N * 2], "int32"),
+    "lci": ("sbuf", [128, LEVELS * KIDS], "int32"),
+    "rci": ("sbuf", [128, LEVELS * KIDS], "int32"),
+    "so": ("sbuf", [128, LEVELS * OFFS], "uint16"),
+    "lo": ("sbuf", [128, LEVELS * KIDS], "uint16"),
+    "ro": ("sbuf", [128, LEVELS * KIDS], "uint16"),
+    "wlq": ("sbuf", [128, 512], F8), "wls": ("sbuf", [128, 512], "uint8"),
+    "wrq": ("sbuf", [128, 512], F8), "wrs": ("sbuf", [128, 512], "uint8"),
+    "vq": ("sbuf", [128, 128], F8), "vs": ("sbuf", [128, 128], "uint8"),
+    "hq": ("sbuf", [128, NODES], F8), "hs": ("sbuf", [128, NODES], "uint8"),
+    "ys": ("sbuf", [128, NODES], "float32"),
+    "psa": ("psum", [128, 2048], "float32"),
+    "psb": ("psum", [128, 2048], "float32"),
+}
+WIDE = {1: LEAVES, 2: BASE + N * CAPP, 3: BASE + 2 * N * CAPP, 4: BASE + 3 * N * CAPP}
+for _t in WIDE:
+    SCRATCH["w%dq" % _t] = ("sbuf", [128, WIDE[_t]], F8)
+    SCRATCH["w%ds" % _t] = ("sbuf", [128, WIDE[_t]], "uint8")
+for _t in (1, 2, 3):
+    SCRATCH["o%dq" % _t] = ("sbuf", [128, SENT], F8)
+    SCRATCH["o%ds" % _t] = ("sbuf", [128, SENT], "uint8")
+    SCRATCH["h%d" % _t] = ("sbuf", [128, 4 * NODES], "bfloat16")
+    for _n in ("l", "r"):
+        SCRATCH["%s%dq" % (_n, _t)] = ("sbuf", [128, NODES], F8)
+        SCRATCH["%s%ds" % (_n, _t)] = ("sbuf", [128, NODES], "uint8")
+
+SEMAPHORES = ["ldx", "ldsn", "ldwl", "ldwr", "ldv", "ldlc", "ldrc", "so1", "so23", "clo", "cro",
+              "qx1", "qx2", "qwl", "qwr", "qv", "own3", "own4a", "own4b", "cp3", "cp4a", "cp4b", "left",
+              "qh", "mmy", "evy", "sty"]
+for _t in (1, 2, 3):
+    SEMAPHORES += ["%s%d" % (_n, _t) for _n in ("poq", "pos", "arq", "ars", "plq", "pls", "prq", "prs", "evv", "evs", "qn")]
+    SEMAPHORES += ["mm%d_%d" % (_t, _i) for _i in range(4)]
+
+
+def plan(topo, cores, s):
+    out = []
+    others = [d for d in range(N) if d != s]
+    big = (s + 1) % N
+    n = 0
+    for k, d in enumerate(others):
+        e = topo.engines(cores[s], cores[d])[:8]
+        halves = (e[0::2], e[1::2])
+        masks = []
+        for h in (0, 1):
+            masks.append(halves[h] if d == big else [halves[1 - h][n]])
+        if d != big:
+            n += 1
+        out.append((d, k, masks[0], masks[1]))
+    return out
+
+
+def bits(es):
+    m = 0
+    for e in es:
+        m |= 1 << e
+    return m
+
+
+def rank_program(g, core, T, topo):
+    rank = T.rank_of(core)
+    if rank is None:
+        return
+    cores = list(T.cores)
+    S = T.sem
+    V, A, E, Y = g.vector, g.scalar, g.tensor, g.sync
+    RELU, COPY = ActivationFunctionType.Relu, ActivationFunctionType.Copy
+
+    def arrivals(which):
+        return sum(len(p[2 + which]) for s in range(N) if s != rank for p in plan(topo, cores, s) if p[0] == rank)
+    NQ, NS = arrivals(0), arrivals(1)
+
+    runs = [(a, b) for a, b in ((0, rank), (rank + 1, N)) if b > a]
+
+    def table(q, out, src, groups, sem):
+        for k in groups:
+            q.dma_start(out[16 * k:16 * k + 16, :], src[:, :]).then_inc(sem, 16)
+    Y.dma_start(T.xt[:], T.x[:]).then_inc(S.ldx, 16)
+    table(A, T.sni, T.sn, range(0, 5), S.ldsn)
+    table(Y, T.sni, T.sn, range(5, 8), S.ldsn)
+    Y.dma_start(T.wlt[:], T.wl[:]).then_inc(S.ldwl, 16)
+    A.dma_start(T.wrt[:], T.wr[:]).then_inc(S.ldwr, 16)
+    table(Y, T.lci, T.lc, range(8), S.ldlc)
+    table(Y, T.rci, T.rc, range(8), S.ldrc)
+    Y.dma_start(T.vt[:], T.v[:]).then_inc(S.ldv, 16)
+
+    def slots_list(t, sem):
+        k = OFFS * (t - 1)
+        for a, b in runs:
+            V.tensor_copy(T.so[:, k:k + 2 * (b - a)], T.sni[:, 2 * N * (t - 1) + 2 * a:2 * N * (t - 1) + 2 * b]).then_inc(sem, 1)
+            k += 2 * (b - a)
+
+    def quant(t, tile, at, n, sem):
+        V.quantize_mx(T["w%dq" % t][:, at:at + n], T["w%ds" % t][:, at:at + n], tile[:]).then_inc(sem, 1)
+
+    def pick_codes(name, n, t, off, a, b, sem):
+        V.tensor_copy(T[name + "q"][:, 0:n].bitcast(dt.uint32),
+                      T["w%dq" % t][:, 0:WIDE[t]].bitcast(dt.uint32).indirect(off[:, a:b])).then_inc(sem, 1)
+
+    def pick_scales(name, n, t, off, a, b, sem):
+        A.activation(T[name + "s"][:, 0:n], T["w%ds" % t][:, 0:WIDE[t]].indirect(off[:, a:b]), COPY).then_inc(sem, 1)
+
+    def bank(t, i):
+        return (T.psa if t % 2 else T.psb)[:, 512 * i:512 * i + NODES]
+
+    V.wait_ge(S.ldsn, 128)
+    slots_list(1, S.so1)
+    V.wait_ge(S.ldx, 16)
+    quant(1, T.xt, 0, LEAVES, S.qx1)
+    V.wait_ge(S.so1, len(runs))
+    V.wait_ge(S.qx1, 1)
+    pick_codes("o1", SENT, 1, T.so, 0, OFFS, S.poq1)
+    quant(2, T.xt, 0, LEAVES, S.qx2)
+    slots_list(2, S.so23)
+    slots_list(3, S.so23)
+    V.wait_ge(S.ldwl, 16)
+    V.quantize_mx(T.wlq[:], T.wls[:], T.wlt[:]).then_inc(S.qwl, 1)
+    V.wait_ge(S.ldwr, 16)
+    V.quantize_mx(T.wrq[:], T.wrs[:], T.wrt[:]).then_inc(S.qwr, 1)
+    V.wait_ge(S.ldlc, 128)
+    V.tensor_copy(T.lo[:], T.lci[:]).then_inc(S.clo, 1)
+    V.wait_ge(S.ldrc, 128)
+    V.tensor_copy(T.ro[:], T.rci[:]).then_inc(S.cro, 1)
+    V.wait_ge(S.qx2, 1)
+    V.wait_ge(S.so23, 2 * len(runs))
+    V.wait_ge(S.clo, 1)
+    V.wait_ge(S.cro, 1)
+    for t in (1, 2, 3):
+        if t == 2:
+            V.wait_ge(S.own3, 2)
+            V.wait_ge(S.cp3, 32 * len(runs))
+        if t == 3:
+            V.wait_ge(S.own4a, 2)
+            V.wait_ge(S.own4b, 1)
+            V.wait_ge(S.cp4a, 32 * len(runs))
+            V.wait_ge(S.cp4b, 32 * len(runs))
+        V.wait_ge(S["arq%d" % t], NQ)
+        pick_codes("l%d" % t, NODES, t + 1, T.lo, KIDS * (t - 1), KIDS * t, S["plq%d" % t])
+        pick_codes("r%d" % t, NODES, t + 1, T.ro, KIDS * (t - 1), KIDS * t, S["prq%d" % t])
+        h = T["h%d" % t]
+        for i in (1, 3):
+            V.wait_ge(S["mm%d_%d" % (t, i)], 1)
+            V.tensor_scalar(h[:, i:4 * NODES:4], bank(t, i), 0.0, 0.05, AluOpType.max, AluOpType.mult).then_inc(S["evv%d" % t], 1)
+        V.wait_ge(S["evs%d" % t], 2)
+        V.wait_ge(S["evv%d" % t], 2)
+        if t < 3:
+            quant(t + 1, h, LEAVES + (t - 1) * NODES, NODES, S["qn%d" % t])
+            V.wait_ge(S["qn%d" % t], 1)
+            pick_codes("o%d" % (t + 1), SENT, t + 1, T.so, OFFS * t, OFFS * (t + 1), S["poq%d" % (t + 1)])
+        if t == 1:
+            quant(3, h, LEAVES, NODES, S.own3)
+            quant(3, T.xt, 0, LEAVES, S.own3)
+            quant(4, h, LEAVES, NODES, S.own4a)
+            quant(4, T.xt, 0, LEAVES, S.own4a)
+            V.wait_ge(S.ldv, 16)
+            V.quantize_mx(T.vq[:], T.vs[:], T.vt[:]).then_inc(S.qv, 1)
+        if t == 2:
+            quant(4, h, LEAVES + NODES, NODES, S.own4b)
+        if t == 3:
+            V.quantize_mx(T.hq[:], T.hs[:], h[:]).then_inc(S.qh, 1)
+            V.wait_ge(S.mmy, 1)
+            V.tensor_copy(T.ys[:], T.psb[:, 0:NODES]).then_inc(S.evy, 1)
+
+    A.wait_ge(S.so1, len(runs))
+    A.wait_ge(S.qx1, 1)
+    pick_scales("o1", SENT, 1, T.so, 0, OFFS, S.pos1)
+    A.wait_ge(S.qx2, 1)
+    A.wait_ge(S.so23, 2 * len(runs))
+    A.wait_ge(S.clo, 1)
+    A.wait_ge(S.cro, 1)
+    for t in (1, 2, 3):
+        if t == 2:
+            A.wait_ge(S.own3, 2)
+            A.wait_ge(S.cp3, 32 * len(runs))
+        if t == 3:
+            A.wait_ge(S.own4a, 2)
+            A.wait_ge(S.own4b, 1)
+            A.wait_ge(S.cp4a, 32 * len(runs))
+            A.wait_ge(S.cp4b, 32 * len(runs))
+        A.wait_ge(S["ars%d" % t], NS)
+        pick_scales("l%d" % t, NODES, t + 1, T.lo, KIDS * (t - 1), KIDS * t, S["pls%d" % t])
+        pick_scales("r%d" % t, NODES, t + 1, T.ro, KIDS * (t - 1), KIDS * t, S["prs%d" % t])
+        h = T["h%d" % t]
+        for i in (0, 2):
+            A.wait_ge(S["mm%d_%d" % (t, i)], 1)
+            A.activation(h[:, i:4 * NODES:4], bank(t, i), RELU, scale=0.05).then_inc(S["evs%d" % t], 1)
+        if t < 3:
+            A.wait_ge(S["qn%d" % t], 1)
+            pick_scales("o%d" % (t + 1), SENT, t + 1, T.so, OFFS * t, OFFS * (t + 1), S["pos%d" % (t + 1)])
+
+    E.wait_ge(S.qwl, 1)
+    for t in (1, 2, 3):
+        E.wait_ge(S["plq%d" % t], 1)
+        E.wait_ge(S["pls%d" % t], 1)
+        for i in range(4):
+            E.matmul_mx(bank(t, i), T.wlq[:, 128 * i:128 * i + 128], T.wls[:, 128 * i:128 * i + 128],
+                        T["l%dq" % t][:], T["l%ds" % t][:], True, False)
+        if t == 1:
+            E.wait_ge(S.qwr, 1)
+        E.wait_ge(S["prq%d" % t], 1)
+        E.wait_ge(S["prs%d" % t], 1)
+        for i in range(4):
+            E.matmul_mx(bank(t, i), T.wrq[:, 128 * i:128 * i + 128], T.wrs[:, 128 * i:128 * i + 128],
+                        T["r%dq" % t][:], T["r%ds" % t][:], False, True).then_inc(S["mm%d_%d" % (t, i)], 1)
+    E.wait_ge(S.qv, 1)
+    E.wait_ge(S.qh, 1)
+    E.matmul_mx(T.psb[:, 0:NODES], T.vq[:], T.vs[:], T.hq[:], T.hs[:], True, True).then_inc(S.mmy, 1)
+
+    calls = 0
+    for t in (1, 2, 3):
+        for which, form in ((0, "q"), (1, "s")):
+            trs = []
+            for d, k, mq, ms in plan(topo, cores, rank):
+                rid, pid, _se = topo.addr(cores[d])
+                at = BASE + ((t - 1) * N + rank) * CAPP
+                src = T["o%d%s" % (t, form)][:, CAPP * k:CAPP * k + CAPP]
+                dst = T["w%d%s" % (t + 1, form)][:, at:at + CAPP]
+                if which == 0:
+                    src, dst = src.bitcast(dt.uint8), dst.bitcast(dt.uint8)
+                es = (mq, ms)[which]
+                calls += len(es)
+                trs.append(RemoteDMATransfer(dst_ids=[DstId(rid=rid, pnc=pid)], dma_engine_mask=bits(es),
+                                             remote_sem=S["ar%s%d" % (form, t)], src=src, dst=dst))
+            g.wait_ge(S["po%s%d" % (form, t)], 1)
+            g.remote_dma_fused(trs, local_sem=S.left)
+    g.wait_ge(S.left, calls)
+
+    def carry(t, src, to, sem):
+        for a, b in runs:
+            lo, hi = BASE + ((t - 1) * N + a) * CAPP, BASE + ((t - 1) * N + b) * CAPP
+            Y.dma_start(T["w%dq" % to][:, lo:hi].bitcast(dt.uint8), T["w%dq" % src][:, lo:hi].bitcast(dt.uint8)).then_inc(sem, 16)
+            Y.dma_start(T["w%ds" % to][:, lo:hi], T["w%ds" % src][:, lo:hi]).then_inc(sem, 16)
+    Y.wait_ge(S.arq1, NQ)
+    Y.wait_ge(S.ars1, NS)
+    carry(1, 2, 3, S.cp3)
+    carry(1, 2, 4, S.cp4a)
+    Y.wait_ge(S.arq2, NQ)
+    Y.wait_ge(S.ars2, NS)
+    carry(2, 3, 4, S.cp4b)
+    Y.wait_ge(S.evy, 1)
+    Y.dma_start(T.y[:], T.ys[:]).then_inc(S.sty, 16)
+    Y.wait_ge(S.sty, 16)

@@ -7,6 +7,7 @@ SENT = (N - 1) * CAPP
 F8 = "float8_e4m3fn_x4"
 KIDS = NODES // 16
 OFFS = SENT // 16
+KEPT = 2 * N * CAPP // 16
 
 SCRATCH = {
     "xt": ("sbuf", [128, 4 * LEAVES], "bfloat16"),
@@ -16,6 +17,11 @@ SCRATCH = {
     "sni": ("sbuf", [128, LEVELS * N * 2], "int32"),
     "lci": ("sbuf", [128, LEVELS * KIDS], "int32"),
     "rci": ("sbuf", [128, LEVELS * KIDS], "int32"),
+    "pi": ("sbuf", [128, KEPT], "int32"),
+    "pm": ("sbuf", [128, KEPT], "int32"),
+    "ci": ("sbuf", [128, KEPT], "int32"),
+    "ki": ("sbuf", [128, KEPT], "int32"),
+    "ko": ("sbuf", [128, KEPT], "uint16"),
     "so": ("sbuf", [128, LEVELS * OFFS], "uint16"),
     "lo": ("sbuf", [128, LEVELS * KIDS], "uint16"),
     "ro": ("sbuf", [128, LEVELS * KIDS], "uint16"),
@@ -39,29 +45,35 @@ for _t in (1, 2, 3):
         SCRATCH["%s%dq" % (_n, _t)] = ("sbuf", [128, NODES], F8)
         SCRATCH["%s%ds" % (_n, _t)] = ("sbuf", [128, NODES], "uint8")
 
-SEMAPHORES = ["ldx", "ldsn", "ldwl", "ldwr", "ldv", "ldlc", "ldrc", "so1", "so23", "clo", "cro",
-              "qx1", "qx2", "qwl", "qwr", "qv", "own3", "own4a", "own4b", "cp3", "cp4a", "cp4b", "left",
+SEMAPHORES = ["ldx", "ldsn", "ldwl", "ldwr", "ldv", "ldlc", "ldrc", "so1", "so1b", "so23", "clo", "cro",
+              "iot", "iom", "ioa", "cko",
+              "qx1", "qx2", "qx34", "qwl", "qwr", "qv", "own3", "own4", "kq3", "ks3", "kq4", "ks4", "left",
               "qh", "mmy", "evy", "sty"]
 for _t in (1, 2, 3):
-    SEMAPHORES += ["%s%d" % (_n, _t) for _n in ("poq", "pos", "arq", "ars", "plq", "pls", "prq", "prs", "evv", "evs", "qn")]
+    SEMAPHORES += ["%s%d" % (_n, _t) for _n in ("paq", "pas", "pbq", "pbs", "arq", "ars", "plq", "pls", "prq", "prs",
+                                                "evv", "evs", "qn")]
     SEMAPHORES += ["mm%d_%d" % (_t, _i) for _i in range(4)]
 
 
+def order(topo, cores, s):
+    me = topo.chip(cores[s])
+    far, near, mate = [], [], []
+    for k in range(1, N):
+        d = (s + k) % N
+        c = topo.chip(cores[d])
+        (mate if topo.mates(me, c) else near if topo.same_plane(me, c) else far).append(d)
+    return far, near + mate
+
+
 def plan(topo, cores, s):
-    out = []
-    others = [d for d in range(N) if d != s]
-    big = (s + 1) % N
-    n = 0
-    for k, d in enumerate(others):
-        e = topo.engines(cores[s], cores[d])[:8]
-        halves = (e[0::2], e[1::2])
-        masks = []
-        for h in (0, 1):
-            masks.append(halves[h] if d == big else [halves[1 - h][n]])
-        if d != big:
-            n += 1
-        out.append((d, k, masks[0], masks[1]))
-    return out
+    far, one = order(topo, cores, s)
+    e = topo.engines(cores[s], cores[far[0]])[:8]
+    a = [(d, k, e[4 * k:4 * k + 4]) for k, d in enumerate(far)]
+
+    def others(big, small):
+        return [(d, len(far) + k, es) for k, (d, es) in enumerate(zip(one, (big, small[:2], small[2:])))]
+    return [("q", "pa", a), ("s", "pa", a),
+            ("q", "pb", others(e[0::2], e[1::2])), ("s", "pb", others(e[1::2], e[0::2]))]
 
 
 def bits(es):
@@ -80,11 +92,17 @@ def rank_program(g, core, T, topo):
     V, A, E, Y = g.vector, g.scalar, g.tensor, g.sync
     RELU, COPY = ActivationFunctionType.Relu, ActivationFunctionType.Copy
 
-    def arrivals(which):
-        return sum(len(p[2 + which]) for s in range(N) if s != rank for p in plan(topo, cores, s) if p[0] == rank)
-    NQ, NS = arrivals(0), arrivals(1)
+    def arrivals(form):
+        return sum(len(es) for s in range(N) if s != rank for f, _p, trs in plan(topo, cores, s) if f == form
+                   for d, _k, es in trs if d == rank)
+    NQ, NS = arrivals("q"), arrivals("s")
 
-    runs = [(a, b) for a, b in ((0, rank), (rank + 1, N)) if b > a]
+    def runs_of(levels):
+        cuts = [-1] + [N * t + rank for t in range(levels)] + [N * levels]
+        return [(a + 1, b) for a, b in zip(cuts, cuts[1:]) if b > a + 1]
+    runs, runs2 = runs_of(1), runs_of(2)
+    far, one = order(topo, cores, rank)
+    CUT = len(far)
 
     def table(q, out, src, groups, sem):
         for k in groups:
@@ -95,38 +113,60 @@ def rank_program(g, core, T, topo):
     Y.dma_start(T.wlt[:], T.wl[:]).then_inc(S.ldwl, 16)
     A.dma_start(T.wrt[:], T.wr[:]).then_inc(S.ldwr, 16)
     table(Y, T.lci, T.lc, range(8), S.ldlc)
-    table(Y, T.rci, T.rc, range(8), S.ldrc)
+    table(A, T.rci, T.rc, range(8), S.ldrc)
     Y.dma_start(T.vt[:], T.v[:]).then_inc(S.ldv, 16)
 
-    def slots_list(t, sem):
-        k = OFFS * (t - 1)
-        for a, b in runs:
-            V.tensor_copy(T.so[:, k:k + 2 * (b - a)], T.sni[:, 2 * N * (t - 1) + 2 * a:2 * N * (t - 1) + 2 * b]).then_inc(sem, 1)
-            k += 2 * (b - a)
+    def slots_list(t, ds, k, sem):
+        for d in ds:
+            at, of = OFFS * (t - 1) + 2 * k, 2 * (N * (t - 1) + d)
+            V.tensor_copy(T.so[:, at:at + 2], T.sni[:, of:of + 2]).then_inc(sem, 1)
+            k += 1
 
     def quant(t, tile, at, n, sem):
         V.quantize_mx(T["w%dq" % t][:, at:at + n], T["w%ds" % t][:, at:at + n], tile[:]).then_inc(sem, 1)
 
-    def pick_codes(name, n, t, off, a, b, sem):
-        V.tensor_copy(T[name + "q"][:, 0:n].bitcast(dt.uint32),
+    def pick_codes(name, at, n, t, off, a, b, sem):
+        V.tensor_copy(T[name + "q"][:, at:at + n].bitcast(dt.uint32),
                       T["w%dq" % t][:, 0:WIDE[t]].bitcast(dt.uint32).indirect(off[:, a:b])).then_inc(sem, 1)
 
-    def pick_scales(name, n, t, off, a, b, sem):
-        A.activation(T[name + "s"][:, 0:n], T["w%ds" % t][:, 0:WIDE[t]].indirect(off[:, a:b]), COPY).then_inc(sem, 1)
+    def pick_scales(name, at, n, t, off, a, b, sem):
+        A.activation(T[name + "s"][:, at:at + n], T["w%ds" % t][:, 0:WIDE[t]].indirect(off[:, a:b]), COPY).then_inc(sem, 1)
+
+    def pick_far(pick, t, sem):
+        pick("o%d" % t, 0, CUT * CAPP, t, T.so, OFFS * (t - 1), OFFS * (t - 1) + 2 * CUT, sem)
+
+    def pick_one(pick, t, sem):
+        pick("o%d" % t, CUT * CAPP, SENT - CUT * CAPP, t, T.so, OFFS * (t - 1) + 2 * CUT, OFFS * t, sem)
+
+    def keep(pick, rs, t, sem):
+        for a, b in rs:
+            pick("w%d" % (t + 1), BASE + a * CAPP, (b - a) * CAPP, t, T.ko, 2 * a, 2 * b, sem)
 
     def bank(t, i):
         return (T.psa if t % 2 else T.psb)[:, 512 * i:512 * i + NODES]
 
+    V.wait_ge(S.iot, 2)
+    V.tensor_scalar(T.pm[:], T.pi[:], 15, None, AluOpType.bitwise_and).then_inc(S.iom, 1)
+    V.wait_ge(S.iom, 1)
+    V.tensor_tensor(T.ki[:], T.pm[:], T.ci[:], AluOpType.add).then_inc(S.ioa, 1)
+    V.wait_ge(S.ioa, 1)
+    V.tensor_copy(T.ko[:], T.ki[:]).then_inc(S.cko, 1)
+
     V.wait_ge(S.ldsn, 128)
-    slots_list(1, S.so1)
+    slots_list(1, far, 0, S.so1)
     V.wait_ge(S.ldx, 16)
     quant(1, T.xt, 0, LEAVES, S.qx1)
-    V.wait_ge(S.so1, len(runs))
+    V.wait_ge(S.so1, CUT)
     V.wait_ge(S.qx1, 1)
-    pick_codes("o1", SENT, 1, T.so, 0, OFFS, S.poq1)
+    pick_far(pick_codes, 1, S.paq1)
+    slots_list(1, one, CUT, S.so1b)
+    V.wait_ge(S.so1b, len(one))
+    pick_one(pick_codes, 1, S.pbq1)
     quant(2, T.xt, 0, LEAVES, S.qx2)
-    slots_list(2, S.so23)
-    slots_list(3, S.so23)
+    quant(3, T.xt, 0, LEAVES, S.qx34)
+    quant(4, T.xt, 0, LEAVES, S.qx34)
+    for t in (2, 3):
+        slots_list(t, far + one, 0, S.so23)
     V.wait_ge(S.ldwl, 16)
     V.quantize_mx(T.wlq[:], T.wls[:], T.wlt[:]).then_inc(S.qwl, 1)
     V.wait_ge(S.ldwr, 16)
@@ -135,22 +175,27 @@ def rank_program(g, core, T, topo):
     V.tensor_copy(T.lo[:], T.lci[:]).then_inc(S.clo, 1)
     V.wait_ge(S.ldrc, 128)
     V.tensor_copy(T.ro[:], T.rci[:]).then_inc(S.cro, 1)
-    V.wait_ge(S.qx2, 1)
-    V.wait_ge(S.so23, 2 * len(runs))
-    V.wait_ge(S.clo, 1)
-    V.wait_ge(S.cro, 1)
-    for t in (1, 2, 3):
+
+    def ready(q, t):
+        if t == 1:
+            q.wait_ge(S.qx2, 1)
+            q.wait_ge(S.qx34, 2)
+            q.wait_ge(S.so23, 2 * (N - 1))
+            q.wait_ge(S.clo, 1)
+            q.wait_ge(S.cro, 1)
+            q.wait_ge(S.cko, 1)
         if t == 2:
-            V.wait_ge(S.own3, 2)
-            V.wait_ge(S.cp3, 32 * len(runs))
+            q.wait_ge(S.own3, 1)
+            q.wait_ge(S.kq3 if q is V else S.ks3, len(runs))
         if t == 3:
-            V.wait_ge(S.own4a, 2)
-            V.wait_ge(S.own4b, 1)
-            V.wait_ge(S.cp4a, 32 * len(runs))
-            V.wait_ge(S.cp4b, 32 * len(runs))
+            q.wait_ge(S.own4, 2)
+            q.wait_ge(S.kq4 if q is V else S.ks4, len(runs2))
+
+    for t in (1, 2, 3):
+        ready(V, t)
         V.wait_ge(S["arq%d" % t], NQ)
-        pick_codes("l%d" % t, NODES, t + 1, T.lo, KIDS * (t - 1), KIDS * t, S["plq%d" % t])
-        pick_codes("r%d" % t, NODES, t + 1, T.ro, KIDS * (t - 1), KIDS * t, S["prq%d" % t])
+        pick_codes("l%d" % t, 0, NODES, t + 1, T.lo, KIDS * (t - 1), KIDS * t, S["plq%d" % t])
+        pick_codes("r%d" % t, 0, NODES, t + 1, T.ro, KIDS * (t - 1), KIDS * t, S["prq%d" % t])
         h = T["h%d" % t]
         for i in (1, 3):
             V.wait_ge(S["mm%d_%d" % (t, i)], 1)
@@ -160,47 +205,44 @@ def rank_program(g, core, T, topo):
         if t < 3:
             quant(t + 1, h, LEAVES + (t - 1) * NODES, NODES, S["qn%d" % t])
             V.wait_ge(S["qn%d" % t], 1)
-            pick_codes("o%d" % (t + 1), SENT, t + 1, T.so, OFFS * t, OFFS * (t + 1), S["poq%d" % (t + 1)])
+            pick_far(pick_codes, t + 1, S["paq%d" % (t + 1)])
+            pick_one(pick_codes, t + 1, S["pbq%d" % (t + 1)])
         if t == 1:
             quant(3, h, LEAVES, NODES, S.own3)
-            quant(3, T.xt, 0, LEAVES, S.own3)
-            quant(4, h, LEAVES, NODES, S.own4a)
-            quant(4, T.xt, 0, LEAVES, S.own4a)
+            keep(pick_codes, runs, 2, S.kq3)
+            quant(4, h, LEAVES, NODES, S.own4)
             V.wait_ge(S.ldv, 16)
             V.quantize_mx(T.vq[:], T.vs[:], T.vt[:]).then_inc(S.qv, 1)
         if t == 2:
-            quant(4, h, LEAVES + NODES, NODES, S.own4b)
+            quant(4, h, LEAVES + NODES, NODES, S.own4)
+            keep(pick_codes, runs2, 3, S.kq4)
         if t == 3:
             V.quantize_mx(T.hq[:], T.hs[:], h[:]).then_inc(S.qh, 1)
             V.wait_ge(S.mmy, 1)
             V.tensor_copy(T.ys[:], T.psb[:, 0:NODES]).then_inc(S.evy, 1)
 
-    A.wait_ge(S.so1, len(runs))
+    A.wait_ge(S.so1, CUT)
     A.wait_ge(S.qx1, 1)
-    pick_scales("o1", SENT, 1, T.so, 0, OFFS, S.pos1)
-    A.wait_ge(S.qx2, 1)
-    A.wait_ge(S.so23, 2 * len(runs))
-    A.wait_ge(S.clo, 1)
-    A.wait_ge(S.cro, 1)
+    pick_far(pick_scales, 1, S.pas1)
+    A.wait_ge(S.so1b, len(one))
+    pick_one(pick_scales, 1, S.pbs1)
     for t in (1, 2, 3):
-        if t == 2:
-            A.wait_ge(S.own3, 2)
-            A.wait_ge(S.cp3, 32 * len(runs))
-        if t == 3:
-            A.wait_ge(S.own4a, 2)
-            A.wait_ge(S.own4b, 1)
-            A.wait_ge(S.cp4a, 32 * len(runs))
-            A.wait_ge(S.cp4b, 32 * len(runs))
+        ready(A, t)
         A.wait_ge(S["ars%d" % t], NS)
-        pick_scales("l%d" % t, NODES, t + 1, T.lo, KIDS * (t - 1), KIDS * t, S["pls%d" % t])
-        pick_scales("r%d" % t, NODES, t + 1, T.ro, KIDS * (t - 1), KIDS * t, S["prs%d" % t])
+        pick_scales("l%d" % t, 0, NODES, t + 1, T.lo, KIDS * (t - 1), KIDS * t, S["pls%d" % t])
+        pick_scales("r%d" % t, 0, NODES, t + 1, T.ro, KIDS * (t - 1), KIDS * t, S["prs%d" % t])
         h = T["h%d" % t]
         for i in (0, 2):
             A.wait_ge(S["mm%d_%d" % (t, i)], 1)
             A.activation(h[:, i:4 * NODES:4], bank(t, i), RELU, scale=0.05).then_inc(S["evs%d" % t], 1)
         if t < 3:
             A.wait_ge(S["qn%d" % t], 1)
-            pick_scales("o%d" % (t + 1), SENT, t + 1, T.so, OFFS * t, OFFS * (t + 1), S["pos%d" % (t + 1)])
+            pick_far(pick_scales, t + 1, S["pas%d" % (t + 1)])
+            pick_one(pick_scales, t + 1, S["pbs%d" % (t + 1)])
+        if t == 1:
+            keep(pick_scales, runs, 2, S.ks3)
+        if t == 2:
+            keep(pick_scales, runs2, 3, S.ks4)
 
     E.wait_ge(S.qwl, 1)
     for t in (1, 2, 3):
@@ -220,37 +262,26 @@ def rank_program(g, core, T, topo):
     E.wait_ge(S.qh, 1)
     E.matmul_mx(T.psb[:, 0:NODES], T.vq[:], T.vs[:], T.hq[:], T.hs[:], True, True).then_inc(S.mmy, 1)
 
-    calls = 0
+    g.iota(T.pi[:], [[0, KEPT]], 0, 1).then_inc(S.iot, 1)
+    g.iota(T.ci[:], [[16, KEPT]], BASE, 0).then_inc(S.iot, 1)
+    left = 0
     for t in (1, 2, 3):
-        for which, form in ((0, "q"), (1, "s")):
+        for form, pick, sends in plan(topo, cores, rank):
             trs = []
-            for d, k, mq, ms in plan(topo, cores, rank):
+            for d, k, es in sends:
                 rid, pid, _se = topo.addr(cores[d])
                 at = BASE + ((t - 1) * N + rank) * CAPP
                 src = T["o%d%s" % (t, form)][:, CAPP * k:CAPP * k + CAPP]
                 dst = T["w%d%s" % (t + 1, form)][:, at:at + CAPP]
-                if which == 0:
+                if form == "q":
                     src, dst = src.bitcast(dt.uint8), dst.bitcast(dt.uint8)
-                es = (mq, ms)[which]
-                calls += len(es)
+                left += len(es)
                 trs.append(RemoteDMATransfer(dst_ids=[DstId(rid=rid, pnc=pid)], dma_engine_mask=bits(es),
                                              remote_sem=S["ar%s%d" % (form, t)], src=src, dst=dst))
-            g.wait_ge(S["po%s%d" % (form, t)], 1)
+            g.wait_ge(S["%s%s%d" % (pick, form, t)], 1)
             g.remote_dma_fused(trs, local_sem=S.left)
-    g.wait_ge(S.left, calls)
+    g.wait_ge(S.left, left)
 
-    def carry(t, src, to, sem):
-        for a, b in runs:
-            lo, hi = BASE + ((t - 1) * N + a) * CAPP, BASE + ((t - 1) * N + b) * CAPP
-            Y.dma_start(T["w%dq" % to][:, lo:hi].bitcast(dt.uint8), T["w%dq" % src][:, lo:hi].bitcast(dt.uint8)).then_inc(sem, 16)
-            Y.dma_start(T["w%ds" % to][:, lo:hi], T["w%ds" % src][:, lo:hi]).then_inc(sem, 16)
-    Y.wait_ge(S.arq1, NQ)
-    Y.wait_ge(S.ars1, NS)
-    carry(1, 2, 3, S.cp3)
-    carry(1, 2, 4, S.cp4a)
-    Y.wait_ge(S.arq2, NQ)
-    Y.wait_ge(S.ars2, NS)
-    carry(2, 3, 4, S.cp4b)
     Y.wait_ge(S.evy, 1)
     Y.dma_start(T.y[:], T.ys[:]).then_inc(S.sty, 16)
     Y.wait_ge(S.sty, 16)

from concourse.bass import DstId, RemoteDMATransfer
from concourse.mybir import dt, AluOpType, ActivationFunctionType

N, LEAVES, NODES, CAPP, LEVELS = 6, 128, 192, 32, 3
BASE = LEAVES + LEVELS * NODES
SENT = (N - 1) * CAPP
F8 = "float8_e4m3fn_x4"
KIDS = NODES // 16
OFFS = SENT // 16
KEPT = 2 * N * CAPP // 16

SCRATCH = {
    "xt": ("sbuf", [128, 4 * LEAVES], "bfloat16"),
    "wlt": ("sbuf", [128, 2048], "bfloat16"),
    "wrt": ("sbuf", [128, 2048], "bfloat16"),
    "vt": ("sbuf", [128, 512], "bfloat16"),
    "sni": ("sbuf", [128, LEVELS * N * 2], "int32"),
    "lci": ("sbuf", [128, LEVELS * KIDS], "int32"),
    "rci": ("sbuf", [128, LEVELS * KIDS], "int32"),
    "pi": ("sbuf", [128, KEPT], "int32"),
    "pm": ("sbuf", [128, KEPT], "int32"),
    "ci": ("sbuf", [128, KEPT], "int32"),
    "ki": ("sbuf", [128, KEPT], "int32"),
    "ko": ("sbuf", [128, KEPT], "uint16"),
    "so": ("sbuf", [128, LEVELS * OFFS], "uint16"),
    "lo": ("sbuf", [128, LEVELS * KIDS], "uint16"),
    "ro": ("sbuf", [128, LEVELS * KIDS], "uint16"),
    "wlq": ("sbuf", [128, 512], F8), "wls": ("sbuf", [128, 512], "uint8"),
    "wrq": ("sbuf", [128, 512], F8), "wrs": ("sbuf", [128, 512], "uint8"),
    "vq": ("sbuf", [128, 128], F8), "vs": ("sbuf", [128, 128], "uint8"),
    "hq": ("sbuf", [128, NODES], F8), "hs": ("sbuf", [128, NODES], "uint8"),
    "ys": ("sbuf", [128, NODES], "float32"),
    "psa": ("psum", [128, 2048], "float32"),
    "psb": ("psum", [128, 2048], "float32"),
}
WIDE = {1: LEAVES, 2: BASE + N * CAPP, 3: BASE + 2 * N * CAPP, 4: BASE + 3 * N * CAPP}
for _t in WIDE:
    SCRATCH["w%dq" % _t] = ("sbuf", [128, WIDE[_t]], F8)
    SCRATCH["w%ds" % _t] = ("sbuf", [128, WIDE[_t]], "uint8")
for _t in (1, 2, 3):
    SCRATCH["o%dq" % _t] = ("sbuf", [128, SENT], F8)
    SCRATCH["o%ds" % _t] = ("sbuf", [128, SENT], "uint8")
    SCRATCH["h%d" % _t] = ("sbuf", [128, 4 * NODES], "bfloat16")
    for _n in ("l", "r"):
        SCRATCH["%s%dq" % (_n, _t)] = ("sbuf", [128, NODES], F8)
        SCRATCH["%s%ds" % (_n, _t)] = ("sbuf", [128, NODES], "uint8")

SEMAPHORES = ["ldx", "ldsn", "ldwl", "ldwr", "ldv", "ldlc", "ldrc", "so1", "so1b", "so23", "clo", "cro",
              "iot", "iom", "ioa", "cko",
              "qx1", "qx2", "qx34", "qwl", "qwr", "qv", "own3", "own4", "kq3", "ks3", "kq4", "ks4", "left",
              "qh", "mmy", "evy", "sty"]
for _t in (1, 2, 3):
    SEMAPHORES += ["%s%d" % (_n, _t) for _n in ("paq", "pas", "pbq", "pbs", "arq", "ars", "plq", "pls", "prq", "prs",
                                                "evv", "evs", "qn")]
    SEMAPHORES += ["mm%d_%d" % (_t, _i) for _i in range(4)]


def order(topo, cores, s):
    me = topo.chip(cores[s])
    far, near, mate = [], [], []
    for k in range(1, N):
        d = (s + k) % N
        c = topo.chip(cores[d])
        (mate if topo.mates(me, c) else near if topo.same_plane(me, c) else far).append(d)
    return far, near + mate


def plan(topo, cores, s):
    far, one = order(topo, cores, s)
    e = topo.engines(cores[s], cores[far[0]])[:8]
    a = [(d, k, e[4 * k:4 * k + 4]) for k, d in enumerate(far)]

    def others(big, small):
        return [(d, len(far) + k, es) for k, (d, es) in enumerate(zip(one, (big, small[:2], small[2:])))]
    return [("q", "pa", a), ("s", "pa", a),
            ("q", "pb", others(e[0::2], e[1::2])), ("s", "pb", others(e[1::2], e[0::2]))]


def bits(es):
    m = 0
    for e in es:
        m |= 1 << e
    return m


def rank_program(g, core, T, topo):
    rank = T.rank_of(core)
    if rank is None:
        return
    cores = list(T.cores)
    S = T.sem
    V, A, E, Y = g.vector, g.scalar, g.tensor, g.sync
    RELU, COPY = ActivationFunctionType.Relu, ActivationFunctionType.Copy

    def arrivals(form):
        return sum(len(es) for s in range(N) if s != rank for f, _p, trs in plan(topo, cores, s) if f == form
                   for d, _k, es in trs if d == rank)
    NQ, NS = arrivals("q"), arrivals("s")

    def runs_of(levels):
        cuts = [-1] + [N * t + rank for t in range(levels)] + [N * levels]
        return [(a + 1, b) for a, b in zip(cuts, cuts[1:]) if b > a + 1]
    runs, runs2 = runs_of(1), runs_of(2)
    far, one = order(topo, cores, rank)
    CUT = len(far)

    def table(q, out, src, groups, sem):
        for k in groups:
            q.dma_start(out[16 * k:16 * k + 16, :], src[:, :]).then_inc(sem, 16)
    Y.dma_start(T.xt[:], T.x[:]).then_inc(S.ldx, 16)
    table(A, T.sni, T.sn, range(0, 5), S.ldsn)
    table(Y, T.sni, T.sn, range(5, 8), S.ldsn)
    Y.dma_start(T.wlt[:], T.wl[:]).then_inc(S.ldwl, 16)
    A.dma_start(T.wrt[:], T.wr[:]).then_inc(S.ldwr, 16)
    table(Y, T.lci, T.lc, range(8), S.ldlc)
    table(A, T.rci, T.rc, range(8), S.ldrc)
    Y.dma_start(T.vt[:], T.v[:]).then_inc(S.ldv, 16)

    def slots_list(t, ds, k, sem):
        for d in ds:
            at, of = OFFS * (t - 1) + 2 * k, 2 * (N * (t - 1) + d)
            V.tensor_copy(T.so[:, at:at + 2], T.sni[:, of:of + 2]).then_inc(sem, 1)
            k += 1

    def quant(t, tile, at, n, sem):
        V.quantize_mx(T["w%dq" % t][:, at:at + n], T["w%ds" % t][:, at:at + n], tile[:]).then_inc(sem, 1)

    def pick_codes(name, at, n, t, off, a, b, sem):
        V.tensor_copy(T[name + "q"][:, at:at + n].bitcast(dt.uint32),
                      T["w%dq" % t][:, 0:WIDE[t]].bitcast(dt.uint32).indirect(off[:, a:b])).then_inc(sem, 1)

    def pick_scales(name, at, n, t, off, a, b, sem):
        A.activation(T[name + "s"][:, at:at + n], T["w%ds" % t][:, 0:WIDE[t]].indirect(off[:, a:b]), COPY).then_inc(sem, 1)

    def pick_far(pick, t, sem):
        pick("o%d" % t, 0, CUT * CAPP, t, T.so, OFFS * (t - 1), OFFS * (t - 1) + 2 * CUT, sem)

    def pick_one(pick, t, sem):
        pick("o%d" % t, CUT * CAPP, SENT - CUT * CAPP, t, T.so, OFFS * (t - 1) + 2 * CUT, OFFS * t, sem)

    def keep(pick, rs, t, sem):
        for a, b in rs:
            pick("w%d" % (t + 1), BASE + a * CAPP, (b - a) * CAPP, t, T.ko, 2 * a, 2 * b, sem)

    def bank(t, i):
        return (T.psa if t % 2 else T.psb)[:, 512 * i:512 * i + NODES]

    V.wait_ge(S.iot, 2)
    V.tensor_scalar(T.pm[:], T.pi[:], 15, None, AluOpType.bitwise_and).then_inc(S.iom, 1)
    V.wait_ge(S.iom, 1)
    V.tensor_tensor(T.ki[:], T.pm[:], T.ci[:], AluOpType.add).then_inc(S.ioa, 1)
    V.wait_ge(S.ioa, 1)
    V.tensor_copy(T.ko[:], T.ki[:]).then_inc(S.cko, 1)

    V.wait_ge(S.ldsn, 128)
    slots_list(1, far, 0, S.so1)
    V.wait_ge(S.ldx, 16)
    quant(1, T.xt, 0, LEAVES, S.qx1)
    V.wait_ge(S.so1, CUT)
    V.wait_ge(S.qx1, 1)
    pick_far(pick_codes, 1, S.paq1)
    slots_list(1, one, CUT, S.so1b)
    V.wait_ge(S.so1b, len(one))
    pick_one(pick_codes, 1, S.pbq1)
    quant(2, T.xt, 0, LEAVES, S.qx2)
    quant(3, T.xt, 0, LEAVES, S.qx34)
    quant(4, T.xt, 0, LEAVES, S.qx34)
    for t in (2, 3):
        slots_list(t, far + one, 0, S.so23)
    V.wait_ge(S.ldwl, 16)
    V.quantize_mx(T.wlq[:], T.wls[:], T.wlt[:]).then_inc(S.qwl, 1)
    V.wait_ge(S.ldwr, 16)
    V.quantize_mx(T.wrq[:], T.wrs[:], T.wrt[:]).then_inc(S.qwr, 1)
    V.wait_ge(S.ldlc, 128)
    V.tensor_copy(T.lo[:], T.lci[:]).then_inc(S.clo, 1)
    V.wait_ge(S.ldrc, 128)
    V.tensor_copy(T.ro[:], T.rci[:]).then_inc(S.cro, 1)

    def ready(q, t):
        if t == 1:
            q.wait_ge(S.qx2, 1)
            q.wait_ge(S.qx34, 2)
            q.wait_ge(S.so23, 2 * (N - 1))
            q.wait_ge(S.clo, 1)
            q.wait_ge(S.cro, 1)
            q.wait_ge(S.cko, 1)
        if t == 2:
            q.wait_ge(S.own3, 1)
            q.wait_ge(S.kq3 if q is V else S.ks3, len(runs))
        if t == 3:
            q.wait_ge(S.own4, 2)
            q.wait_ge(S.kq4 if q is V else S.ks4, len(runs2))

    for t in (1, 2, 3):
        ready(V, t)
        V.wait_ge(S["arq%d" % t], NQ)
        pick_codes("l%d" % t, 0, NODES, t + 1, T.lo, KIDS * (t - 1), KIDS * t, S["plq%d" % t])
        pick_codes("r%d" % t, 0, NODES, t + 1, T.ro, KIDS * (t - 1), KIDS * t, S["prq%d" % t])
        h = T["h%d" % t]
        for i in (1, 3):
            V.wait_ge(S["mm%d_%d" % (t, i)], 1)
            V.tensor_scalar(h[:, i:4 * NODES:4], bank(t, i), 0.0, 0.05, AluOpType.max, AluOpType.mult).then_inc(S["evv%d" % t], 1)
        V.wait_ge(S["evs%d" % t], 2)
        V.wait_ge(S["evv%d" % t], 2)
        if t < 3:
            quant(t + 1, h, LEAVES + (t - 1) * NODES, NODES, S["qn%d" % t])
            V.wait_ge(S["qn%d" % t], 1)
            pick_far(pick_codes, t + 1, S["paq%d" % (t + 1)])
            pick_one(pick_codes, t + 1, S["pbq%d" % (t + 1)])
        if t == 1:
            quant(3, h, LEAVES, NODES, S.own3)
            keep(pick_codes, runs, 2, S.kq3)
            quant(4, h, LEAVES, NODES, S.own4)
            V.wait_ge(S.ldv, 16)
            V.quantize_mx(T.vq[:], T.vs[:], T.vt[:]).then_inc(S.qv, 1)
        if t == 2:
            quant(4, h, LEAVES + NODES, NODES, S.own4)
            keep(pick_codes, runs2, 3, S.kq4)
        if t == 3:
            V.quantize_mx(T.hq[:], T.hs[:], h[:]).then_inc(S.qh, 1)
            V.wait_ge(S.mmy, 1)
            V.tensor_copy(T.ys[:], T.psb[:, 0:NODES]).then_inc(S.evy, 1)

    A.wait_ge(S.so1, CUT)
    A.wait_ge(S.qx1, 1)
    pick_far(pick_scales, 1, S.pas1)
    A.wait_ge(S.so1b, len(one))
    pick_one(pick_scales, 1, S.pbs1)
    for t in (1, 2, 3):
        ready(A, t)
        A.wait_ge(S["ars%d" % t], NS)
        pick_scales("l%d" % t, 0, NODES, t + 1, T.lo, KIDS * (t - 1), KIDS * t, S["pls%d" % t])
        pick_scales("r%d" % t, 0, NODES, t + 1, T.ro, KIDS * (t - 1), KIDS * t, S["prs%d" % t])
        h = T["h%d" % t]
        for i in (0, 2):
            A.wait_ge(S["mm%d_%d" % (t, i)], 1)
            A.activation(h[:, i:4 * NODES:4], bank(t, i), RELU, scale=0.05).then_inc(S["evs%d" % t], 1)
        if t < 3:
            A.wait_ge(S["qn%d" % t], 1)
            pick_far(pick_scales, t + 1, S["pas%d" % (t + 1)])
            pick_one(pick_scales, t + 1, S["pbs%d" % (t + 1)])
        if t == 1:
            keep(pick_scales, runs, 2, S.ks3)
        if t == 2:
            keep(pick_scales, runs2, 3, S.ks4)

    E.wait_ge(S.qwl, 1)
    for t in (1, 2, 3):
        E.wait_ge(S["plq%d" % t], 1)
        E.wait_ge(S["pls%d" % t], 1)
        for i in range(4):
            E.matmul_mx(bank(t, i), T.wlq[:, 128 * i:128 * i + 128], T.wls[:, 128 * i:128 * i + 128],
                        T["l%dq" % t][:], T["l%ds" % t][:], True, False)
        if t == 1:
            E.wait_ge(S.qwr, 1)
        E.wait_ge(S["prq%d" % t], 1)
        E.wait_ge(S["prs%d" % t], 1)
        for i in range(4):
            E.matmul_mx(bank(t, i), T.wrq[:, 128 * i:128 * i + 128], T.wrs[:, 128 * i:128 * i + 128],
                        T["r%dq" % t][:], T["r%ds" % t][:], False, True).then_inc(S["mm%d_%d" % (t, i)], 1)
    E.wait_ge(S.qv, 1)
    E.wait_ge(S.qh, 1)
    E.matmul_mx(T.psb[:, 0:NODES], T.vq[:], T.vs[:], T.hq[:], T.hs[:], True, True).then_inc(S.mmy, 1)

    g.iota(T.pi[:], [[0, KEPT]], 0, 1).then_inc(S.iot, 1)
    g.iota(T.ci[:], [[16, KEPT]], BASE, 0).then_inc(S.iot, 1)
    left = 0
    for t in (1, 2, 3):
        for form, pick, sends in plan(topo, cores, rank):
            trs = []
            for d, k, es in sends:
                rid, pid, _se = topo.addr(cores[d])
                at = BASE + ((t - 1) * N + rank) * CAPP
                src = T["o%d%s" % (t, form)][:, CAPP * k:CAPP * k + CAPP]
                dst = T["w%d%s" % (t + 1, form)][:, at:at + CAPP]
                if form == "q":
                    src, dst = src.bitcast(dt.uint8), dst.bitcast(dt.uint8)
                left += len(es)
                trs.append(RemoteDMATransfer(dst_ids=[DstId(rid=rid, pnc=pid)], dma_engine_mask=bits(es),
                                             remote_sem=S["ar%s%d" % (form, t)], src=src, dst=dst))
            g.wait_ge(S["%s%s%d" % (pick, form, t)], 1)
            g.remote_dma_fused(trs, local_sem=S.left)
    g.wait_ge(S.left, left)

    Y.wait_ge(S.evy, 1)
    Y.dma_start(T.y[:], T.ys[:]).then_inc(S.sty, 16)
    Y.wait_ge(S.sty, 16)
